import numpy as np, ml_dtypes
CORES = [7,15,23,39,47,63,71,79,87,95,119,127]
N = 12
S, B = 2, 512
def setup_inputs(rng):
    return {"x": rng.standard_normal((N, 128, S * B), dtype=np.float32).astype(ml_dtypes.bfloat16), "gate": (0.9375 + 0.03125 * rng.standard_normal((N, 128, S * B), dtype=np.float32)).astype(ml_dtypes.bfloat16)}
def setup_inputs_big(rng):
    d = setup_inputs(rng)
    for k in ("x",): d[k] = (d[k].astype(np.float32) * 1048576.0).astype(d[k].dtype)
    return d
def setup_inputs_small(rng):
    d = setup_inputs(rng)
    for k in ("x",): d[k] = (d[k].astype(np.float32) * (1 / 1048576.0)).astype(d[k].dtype)
    return d
def setup_inputs_apart(rng):
    d = setup_inputs(rng)
    f = (10.0 ** rng.permutation(np.linspace(-1.5, 1.5, N))).astype(np.float32).reshape(N, 1, 1)
    for k in ("x",): d[k] = (d[k].astype(np.float32) * f).astype(d[k].dtype)
    return d
def reference(x, gate):
    X, GATE = x.astype(np.float64), gate.astype(np.float64)
    y = np.zeros((N, 128, S * B)); h = np.zeros((128, B))
    for r in range(N):
        for s in range(S):
            h = GATE[r][:, B * s:B * s + B] * h + X[r][:, B * s:B * s + B]
            y[r][:, B * s:B * s + B] = h
    return {"y": y.astype(ml_dtypes.bfloat16)}

@@ -1,0 +1,176 @@
+from concourse.bass import DstId, RemoteDMATransfer
+from concourse.mybir import AluOpType
+
+N = 12
+B = 512
+J = 8
+W = B // J
+FIRST = 3
+
+SCRATCH = {
+    "G": ("sbuf", [128, 2 * B], "bfloat16"),
+    "X": ("sbuf", [128, 2 * B], "bfloat16"),
+    "AB": ("sbuf", [128, J, 2 * W], "bfloat16"),
+    "L": ("sbuf", [128, N - 1, 2 * W], "bfloat16"),
+    "HS": ("sbuf", [128, N, W], "bfloat16"),
+    "HL": ("sbuf", [128, B], "bfloat16"),
+    "Y": ("sbuf", [128, 2 * B], "bfloat16"),
+    "g1p": ("psum", [128, B], "float32"),
+    "g0p": ("psum", [128, B], "float32"),
+    "Ap": ("psum", [128, B], "float32"),
+    "tp": ("psum", [128, B], "float32"),
+    "t0": ("psum", [128, B], "float32"),
+    "t1": ("psum", [128, B], "float32"),
+    "ts": ("psum", [128, W], "float32"),
+}
+SEMAPHORES = ["lg0", "lg1", "lx0", "lx1", "vs", "hs", "snt", "st"] + ["a%d" % s for s in range(N - 1)]
+
+
+def rank_program(g, core, T, topo):
+    r = T.rank_of(core)
+    if r is None:
+        return
+    S = T.sem
+    v = g.vector
+    owners = list(range(FIRST, FIRST + J))
+    nv = [0]
+    sent = [0]
+
+    def vcall(make):
+        if nv[0]:
+            v.wait_ge(S.vs, nv[0])
+        make().then_inc(S.vs, 1)
+        nv[0] += 1
+        return nv[0]
+
+    def mul(out, a, b):
+        return vcall(lambda: v.tensor_tensor(out=out, in0=a, in1=b, op=AluOpType.mult))
+
+    def add(out, a, b):
+        return vcall(lambda: v.tensor_tensor(out=out, in0=a, in1=b, op=AluOpType.add))
+
+    def copy(out, a):
+        return vcall(lambda: v.tensor_copy(out=out, in_=a))
+
+    def groups(dsts, per):
+        m = -1
+        for d in dsts:
+            assert topo.may_write(core, T.cores[d])
+            m &= topo.mask(core, T.cores[d])
+        e = [1 << i for i in range(m.bit_length()) if (m >> i) & 1]
+        assert per * len(dsts) <= len(e)
+        return [sum(e[i * per:(i + 1) * per]) for i in range(len(dsts))]
+
+    def fused(items, per, sem):
+        masks = groups([d for d, _, _ in items], per)
+        tr = []
+        for (d, src, dst), m in zip(items, masks):
+            rid, pid, _ = topo.addr(T.cores[d])
+            tr.append(RemoteDMATransfer(dst_ids=[DstId(rid=rid, pnc=pid)], dma_engine_mask=m, remote_sem=sem,
+                                        src=src, dst=dst))
+            sent[0] += per
+        g.remote_dma_fused(tr, local_sem=S.snt)
+
+    def whole(d, src):
+        c = T.cores[d]
+        assert topo.may_write(core, c)
+        m = topo.mask(core, c)
+        rid, pid, _ = topo.addr(c)
+        g.remote_dma(out_ap=T.HL[:, :], in_ap=src, remote_sem=S.hs, local_sem=S.snt, pid=pid, routing_id=rid,
+                     dma_engine_mask=m)
+        n = bin(m).count("1")
+        sent[0] += n
+        return n
+
+    def width(src_rank, dst_rank):
+        return bin(topo.mask(T.cores[src_rank], T.cores[dst_rank])).count("1")
+
+    g0, g1 = T.G[:, 0:B], T.G[:, B:2 * B]
+    x0, x1 = T.X[:, 0:B], T.X[:, B:2 * B]
+    y0, y1 = T.Y[:, 0:B], T.Y[:, B:2 * B]
+
+    if r == 0:
+        g.sync.dma_start(out=g1, in_=T.gate[:, B:2 * B]).then_inc(S.lg1, 16)
+        g.scalar.dma_start(out=x0, in_=T.x[:, 0:B]).then_inc(S.lx0, 16)
+        g.sync.dma_start(out=x1, in_=T.x[:, B:2 * B]).then_inc(S.lx1, 16)
+        g.scalar.dma_start(out=T.y[:, 0:B], in_=T.x[:, 0:B]).then_inc(S.st, 16)
+        v.wait_ge(S.lg1, 16)
+        copy(T.g1p[:, :], g1)
+        v.wait_ge(S.lx0, 16)
+        mul(T.tp[:, :], T.g1p[:, :], x0)
+        v.wait_ge(S.lx1, 16)
+        n_b = add(y1, T.tp[:, :], x1)
+        g.wait_ge(S.vs, n_b)
+        fused([(o, T.Y[:, B + W * k:B + W * (k + 1)], T.L[:, 0, W:2 * W]) for k, o in enumerate(owners)], 1, S.a0)
+        whole(1, y1)
+        g.sync.wait_ge(S.vs, n_b)
+        g.sync.dma_start(out=T.y[:, B:2 * B], in_=y1).then_inc(S.st, 16)
+        g.wait_ge(S.snt, sent[0])
+        g.wait_ge(S.st, 32)
+        return
+
+    g.sync.dma_start(out=g1, in_=T.gate[:, B:2 * B]).then_inc(S.lg1, 16)
+    g.scalar.dma_start(out=g0, in_=T.gate[:, 0:B]).then_inc(S.lg0, 16)
+    g.sync.dma_start(out=x0, in_=T.x[:, 0:B]).then_inc(S.lx0, 16)
+    g.scalar.dma_start(out=x1, in_=T.x[:, B:2 * B]).then_inc(S.lx1, 16)
+
+    A_il, b_il = T.AB[:, :, 0:W], T.AB[:, :, W:2 * W]
+    v.wait_ge(S.lg1, 16)
+    copy(T.g1p[:, :], g1)
+    v.wait_ge(S.lg0, 16)
+    mul(A_il, T.g1p[:, :], g0)
+    v.wait_ge(S.lx0, 16)
+    mul(T.tp[:, :], T.g1p[:, :], x0)
+    v.wait_ge(S.lx1, 16)
+    n_ab = add(b_il, T.tp[:, :], x1)
+
+    if r < N - 1:
+        g.wait_ge(S.vs, n_ab)
+        fused([(o, T.AB[:, k, :], T.L[:, r, :]) for k, o in enumerate(owners) if o != r], 1, S["a%d" % r])
+
+    copy(T.g0p[:, :], g0)
+    mul(T.Ap[:, :], T.g1p[:, :], g0)
+
+    if r in owners:
+        k = r - FIRST
+        mine = T.HL[:, W * k:W * (k + 1)]
+        ready = {}
+        v.wait_ge(S.a0, 1)
+        prev = T.L[:, 0, W:2 * W]
+        for s in range(1, N - 1):
+            if s == r:
+                a_s, b_s = T.AB[:, k, 0:W], T.AB[:, k, W:2 * W]
+            else:
+                v.wait_ge(S["a%d" % s], 1)
+                a_s, b_s = T.L[:, s, 0:W], T.L[:, s, W:2 * W]
+            mul(T.ts[:, :], a_s, prev)
+            prev = mine if s + 1 == r else T.HS[:, s + 1, :]
+            ready[s + 1] = add(prev, T.ts[:, :], b_s)
+        dsts = [d for d in range(FIRST, N) if d != r]
+        for part in (dsts[:len(dsts) // 2], dsts[len(dsts) // 2:]):
+            g.wait_ge(S.vs, ready[part[-1]])
+            fused([(d, T.HS[:, d, :], mine) for d in part], 2, S.hs)
+
+    if r < FIRST:
+        v.wait_ge(S.hs, width(r - 1, r))
+    else:
+        v.wait_ge(S.hs, 2 * len([o for o in owners if o != r]))
+    if r + 1 < FIRST:
+        mul(T.t1[:, :], T.Ap[:, :], T.HL[:, :])
+        n_y1 = add(y1, T.t1[:, :], b_il)
+        g.wait_ge(S.vs, n_y1)
+        whole(r + 1, y1)
+        mul(T.t0[:, :], T.g0p[:, :], T.HL[:, :])
+        n_y0 = add(y0, T.t0[:, :], x0)
+    else:
+        mul(T.t0[:, :], T.g0p[:, :], T.HL[:, :])
+        n_y0 = add(y0, T.t0[:, :], x0)
+        mul(T.t1[:, :], T.Ap[:, :], T.HL[:, :])
+        n_y1 = add(y1, T.t1[:, :], b_il)
+    g.sync.wait_ge(S.vs, n_y0)
+    g.sync.dma_start(out=T.y[:, 0:B], in_=y0).then_inc(S.st, 16)
+    g.scalar.wait_ge(S.vs, n_y1)
+    g.scalar.dma_start(out=T.y[:, B:2 * B], in_=y1).then_inc(S.st, 16)
+    if sent[0]:
+        g.wait_ge(S.snt, sent[0])
+    g.wait_ge(S.st, 32)

@@ -3,174 +3,126 @@ from concourse.mybir import AluOpType
 
 N = 12
 B = 512
-J = 8
-W = B // J
-FIRST = 3
+CORES_ALL = 128
+J = 32
+R = 128 // J
+SLOT = 32
+GRP = 8
 
 SCRATCH = {
-    "G": ("sbuf", [128, 2 * B], "bfloat16"),
-    "X": ("sbuf", [128, 2 * B], "bfloat16"),
-    "AB": ("sbuf", [128, J, 2 * W], "bfloat16"),
-    "L": ("sbuf", [128, N - 1, 2 * W], "bfloat16"),
-    "HS": ("sbuf", [128, N, W], "bfloat16"),
-    "HL": ("sbuf", [128, B], "bfloat16"),
-    "Y": ("sbuf", [128, 2 * B], "bfloat16"),
-    "g1p": ("psum", [128, B], "float32"),
-    "g0p": ("psum", [128, B], "float32"),
-    "Ap": ("psum", [128, B], "float32"),
-    "tp": ("psum", [128, B], "float32"),
-    "t0": ("psum", [128, B], "float32"),
-    "t1": ("psum", [128, B], "float32"),
-    "ts": ("psum", [128, W], "float32"),
+    "XG": ("dram", [J, 128, 64], "bfloat16"),
+    "D": ("dram", [N, 128, 64], "bfloat16"),
+    "YS": ("dram", [N, 128, 32], "bfloat16"),
+    "YD": ("dram", [J, 128, 32], "bfloat16"),
+    "Gp": ("sbuf", [128, B], "bfloat16"),
+    "Xp": ("sbuf", [128, B], "bfloat16"),
+    "Gf": ("sbuf", [128, B], "bfloat16"),
+    "Xf": ("sbuf", [128, B], "bfloat16"),
+    "Hf": ("sbuf", [128, B], "bfloat16"),
+    "Hp": ("sbuf", [128, B], "bfloat16"),
 }
-SEMAPHORES = ["lg0", "lg1", "lx0", "lx1", "vs", "hs", "snt", "st"] + ["a%d" % s for s in range(N - 1)]
+SEMAPHORES = ["l0", "l1", "arr", "ms", "lg", "lx", "vs", "so", "snt", "ha", "hb", "st"]
+
+
+def owner_cores(T, topo):
+    cores = list(range(CORES_ALL))
+    chips = sorted({topo.chip(c) for c in cores})
+    dies = sorted({topo.die(c) for c in cores})
+    out = []
+    for d in dies:
+        for ch in chips:
+            ok = [c for c in cores if topo.chip(c) == ch and topo.die(c) == d and c not in T.cores
+                  and all(topo.may_write(c, t) for t in T.cores)]
+            out.append(ok[0])
+    assert len(out) == J
+    return out
+
+
+def round2_plan(k):
+    order = [(k + j) % N for j in range(N)]
+    return [[(d, 1) for d in order[:8]], [(d, 2) for d in order[8:]]]
 
 
 def rank_program(g, core, T, topo):
-    r = T.rank_of(core)
-    if r is None:
-        return
     S = T.sem
-    v = g.vector
-    owners = list(range(FIRST, FIRST + J))
-    nv = [0]
+    owners = owner_cores(T, topo)
+    r = T.rank_of(core)
     sent = [0]
 
-    def vcall(make):
-        if nv[0]:
-            v.wait_ge(S.vs, nv[0])
-        make().then_inc(S.vs, 1)
-        nv[0] += 1
-        return nv[0]
-
-    def mul(out, a, b):
-        return vcall(lambda: v.tensor_tensor(out=out, in0=a, in1=b, op=AluOpType.mult))
-
-    def add(out, a, b):
-        return vcall(lambda: v.tensor_tensor(out=out, in0=a, in1=b, op=AluOpType.add))
-
-    def copy(out, a):
-        return vcall(lambda: v.tensor_copy(out=out, in_=a))
-
-    def groups(dsts, per):
+    def fused(items, sem_of):
         m = -1
-        for d in dsts:
-            assert topo.may_write(core, T.cores[d])
-            m &= topo.mask(core, T.cores[d])
+        for c, _, _, _ in items:
+            assert topo.may_write(core, c)
+            m &= topo.mask(core, c)
         e = [1 << i for i in range(m.bit_length()) if (m >> i) & 1]
-        assert per * len(dsts) <= len(e)
-        return [sum(e[i * per:(i + 1) * per]) for i in range(len(dsts))]
-
-    def fused(items, per, sem):
-        masks = groups([d for d, _, _ in items], per)
-        tr = []
-        for (d, src, dst), m in zip(items, masks):
-            rid, pid, _ = topo.addr(T.cores[d])
-            tr.append(RemoteDMATransfer(dst_ids=[DstId(rid=rid, pnc=pid)], dma_engine_mask=m, remote_sem=sem,
-                                        src=src, dst=dst))
-            sent[0] += per
+        tr, at = [], 0
+        for i, (c, src, dst, n) in enumerate(items):
+            rid, pid, _ = topo.addr(c)
+            tr.append(RemoteDMATransfer(dst_ids=[DstId(rid=rid, pnc=pid)], dma_engine_mask=sum(e[at:at + n]),
+                                        remote_sem=sem_of(i), src=src, dst=dst))
+            at += n
+            sent[0] += n
+        assert at <= len(e)
         g.remote_dma_fused(tr, local_sem=S.snt)
 
-    def whole(d, src):
-        c = T.cores[d]
-        assert topo.may_write(core, c)
-        m = topo.mask(core, c)
-        rid, pid, _ = topo.addr(c)
-        g.remote_dma(out_ap=T.HL[:, :], in_ap=src, remote_sem=S.hs, local_sem=S.snt, pid=pid, routing_id=rid,
-                     dma_engine_mask=m)
-        n = bin(m).count("1")
-        sent[0] += n
-        return n
+    if r is not None:
+        turn = r % (J // GRP)
+        half_k, half_p = J // 2, 64
+        for j in range(2):
+            h = ((2 * j) ^ turn) // 2
+            ks, ps = slice(half_k * h, half_k * (h + 1)), slice(half_p * h, half_p * (h + 1))
+            g.sync.dma_start(out=T.XG[ks, 0:64, :], in_=T.gate[ps, :]).then_inc(S["l%d" % j], 16)
+            g.scalar.dma_start(out=T.XG[ks, 64:128, :], in_=T.x[ps, :]).then_inc(S["l%d" % j], 16)
+        for j in range(J // GRP):
+            if j % 2 == 0:
+                g.wait_ge(S["l%d" % (j // 2)], 32)
+            q = j ^ turn
+            fused([(owners[k], T.XG[k], T.D[r], 1) for k in range(GRP * q, GRP * (q + 1))], lambda i: S.arr)
 
-    def width(src_rank, dst_rank):
-        return bin(topo.mask(T.cores[src_rank], T.cores[dst_rank])).count("1")
+        def due(ks):
+            return sum(n for k in ks for call in round2_plan(k) for d, n in call if d == r)
 
-    g0, g1 = T.G[:, 0:B], T.G[:, B:2 * B]
-    x0, x1 = T.X[:, 0:B], T.X[:, B:2 * B]
-    y0, y1 = T.Y[:, 0:B], T.Y[:, B:2 * B]
-
-    if r == 0:
-        g.sync.dma_start(out=g1, in_=T.gate[:, B:2 * B]).then_inc(S.lg1, 16)
-        g.scalar.dma_start(out=x0, in_=T.x[:, 0:B]).then_inc(S.lx0, 16)
-        g.sync.dma_start(out=x1, in_=T.x[:, B:2 * B]).then_inc(S.lx1, 16)
-        g.scalar.dma_start(out=T.y[:, 0:B], in_=T.x[:, 0:B]).then_inc(S.st, 16)
-        v.wait_ge(S.lg1, 16)
-        copy(T.g1p[:, :], g1)
-        v.wait_ge(S.lx0, 16)
-        mul(T.tp[:, :], T.g1p[:, :], x0)
-        v.wait_ge(S.lx1, 16)
-        n_b = add(y1, T.tp[:, :], x1)
-        g.wait_ge(S.vs, n_b)
-        fused([(o, T.Y[:, B + W * k:B + W * (k + 1)], T.L[:, 0, W:2 * W]) for k, o in enumerate(owners)], 1, S.a0)
-        whole(1, y1)
-        g.sync.wait_ge(S.vs, n_b)
-        g.sync.dma_start(out=T.y[:, B:2 * B], in_=y1).then_inc(S.st, 16)
+        g.sync.wait_ge(S.ha, due(range(0, half_k)))
+        g.sync.dma_start(out=T.y[0:half_p, :], in_=T.YD[0:half_k, :, :]).then_inc(S.st, 16)
+        g.scalar.wait_ge(S.hb, due(range(half_k, J)))
+        g.scalar.dma_start(out=T.y[half_p:128, :], in_=T.YD[half_k:J, :, :]).then_inc(S.st, 16)
         g.wait_ge(S.snt, sent[0])
         g.wait_ge(S.st, 32)
         return
 
-    g.sync.dma_start(out=g1, in_=T.gate[:, B:2 * B]).then_inc(S.lg1, 16)
-    g.scalar.dma_start(out=g0, in_=T.gate[:, 0:B]).then_inc(S.lg0, 16)
-    g.sync.dma_start(out=x0, in_=T.x[:, 0:B]).then_inc(S.lx0, 16)
-    g.scalar.dma_start(out=x1, in_=T.x[:, B:2 * B]).then_inc(S.lx1, 16)
+    if core not in owners:
+        return
 
-    A_il, b_il = T.AB[:, :, 0:W], T.AB[:, :, W:2 * W]
-    v.wait_ge(S.lg1, 16)
-    copy(T.g1p[:, :], g1)
-    v.wait_ge(S.lg0, 16)
-    mul(A_il, T.g1p[:, :], g0)
-    v.wait_ge(S.lx0, 16)
-    mul(T.tp[:, :], T.g1p[:, :], x0)
-    v.wait_ge(S.lx1, 16)
-    n_ab = add(b_il, T.tp[:, :], x1)
-
-    if r < N - 1:
-        g.wait_ge(S.vs, n_ab)
-        fused([(o, T.AB[:, k, :], T.L[:, r, :]) for k, o in enumerate(owners) if o != r], 1, S["a%d" % r])
-
-    copy(T.g0p[:, :], g0)
-    mul(T.Ap[:, :], T.g1p[:, :], g0)
-
-    if r in owners:
-        k = r - FIRST
-        mine = T.HL[:, W * k:W * (k + 1)]
-        ready = {}
-        v.wait_ge(S.a0, 1)
-        prev = T.L[:, 0, W:2 * W]
-        for s in range(1, N - 1):
-            if s == r:
-                a_s, b_s = T.AB[:, k, 0:W], T.AB[:, k, W:2 * W]
-            else:
-                v.wait_ge(S["a%d" % s], 1)
-                a_s, b_s = T.L[:, s, 0:W], T.L[:, s, W:2 * W]
-            mul(T.ts[:, :], a_s, prev)
-            prev = mine if s + 1 == r else T.HS[:, s + 1, :]
-            ready[s + 1] = add(prev, T.ts[:, :], b_s)
-        dsts = [d for d in range(FIRST, N) if d != r]
-        for part in (dsts[:len(dsts) // 2], dsts[len(dsts) // 2:]):
-            g.wait_ge(S.vs, ready[part[-1]])
-            fused([(d, T.HS[:, d, :], mine) for d in part], 2, S.hs)
-
-    if r < FIRST:
-        v.wait_ge(S.hs, width(r - 1, r))
-    else:
-        v.wait_ge(S.hs, 2 * len([o for o in owners if o != r]))
-    if r + 1 < FIRST:
-        mul(T.t1[:, :], T.Ap[:, :], T.HL[:, :])
-        n_y1 = add(y1, T.t1[:, :], b_il)
-        g.wait_ge(S.vs, n_y1)
-        whole(r + 1, y1)
-        mul(T.t0[:, :], T.g0p[:, :], T.HL[:, :])
-        n_y0 = add(y0, T.t0[:, :], x0)
-    else:
-        mul(T.t0[:, :], T.g0p[:, :], T.HL[:, :])
-        n_y0 = add(y0, T.t0[:, :], x0)
-        mul(T.t1[:, :], T.Ap[:, :], T.HL[:, :])
-        n_y1 = add(y1, T.t1[:, :], b_il)
-    g.sync.wait_ge(S.vs, n_y0)
-    g.sync.dma_start(out=T.y[:, 0:B], in_=y0).then_inc(S.st, 16)
-    g.scalar.wait_ge(S.vs, n_y1)
-    g.scalar.dma_start(out=T.y[:, B:2 * B], in_=y1).then_inc(S.st, 16)
-    if sent[0]:
-        g.wait_ge(S.snt, sent[0])
-    g.wait_ge(S.st, 32)
+    k = owners.index(core)
+    v = g.vector
+    used = 2 * N
+    v.memset(T.Gp[:, :], 0.0).then_inc(S.ms, 1)
+    v.memset(T.Xp[:, :], 0.0).then_inc(S.ms, 1)
+    queues = (g.sync, g.scalar)
+    for q in queues:
+        q.wait_ge(S.ms, 2)
+        q.wait_ge(S.arr, N)
+    for t, (buf, sem) in enumerate(((T.Gp, S.lg), (T.Xp, S.lx))):
+        for p in range(R):
+            queues[p % 2].dma_start(out=buf[SLOT * p:SLOT * p + used, :],
+                                    in_=T.D[:, 64 * t + 16 * p:64 * t + 16 * (p + 1), :]).then_inc(sem, 16)
+    v.wait_ge(S.ms, 2)
+    v.wait_ge(S.lg, 16 * R)
+    v.transpose(out=T.Gf[:, :], in_=T.Gp[:, :]).then_inc(S.vs, 1)
+    v.wait_ge(S.lx, 16 * R)
+    v.transpose(out=T.Xf[:, :], in_=T.Xp[:, :]).then_inc(S.vs, 1)
+    v.wait_ge(S.vs, 2)
+    v.tensor_tensor_scan(out=T.Hf[:, :], data0=T.Gf[:, :], data1=T.Xf[:, :], initial=0.0,
+                         op0=AluOpType.mult, op1=AluOpType.add).then_inc(S.vs, 1)
+    v.wait_ge(S.vs, 3)
+    v.transpose(out=T.Hp[:, :], in_=T.Hf[:, :]).then_inc(S.vs, 1)
+    for q in queues:
+        q.wait_ge(S.vs, 4)
+    for p in range(R):
+        queues[p % 2].dma_start(out=T.YS[:, 32 * p:32 * (p + 1), :],
+                                in_=T.Hp[SLOT * p:SLOT * p + used, :]).then_inc(S.so, 16)
+    g.wait_ge(S.so, 16 * R)
+    land = S.ha if k < J // 2 else S.hb
+    for call in round2_plan(k):
+        fused([(T.cores[d], T.YS[d], T.YD[k], n) for d, n in call], lambda i: land)
+    g.wait_ge(S.snt, sent[0])

@@ -5,23 +5,25 @@ N = 12
 B = 512
 CORES_ALL = 128
 J = 32
+WAVES = 2
+OWN = J // WAVES
 R = 128 // J
 SLOT = 32
 GRP = 8
 
 SCRATCH = {
-    "XG": ("dram", [J, 128, 64], "bfloat16"),
-    "D": ("dram", [N, 128, 64], "bfloat16"),
-    "YS": ("dram", [N, 128, 32], "bfloat16"),
+    "SG": ("dram", [J, 128, 32], "bfloat16"),
+    "SX": ("dram", [J, 128, 32], "bfloat16"),
+    "DG": ("dram", [WAVES * N, 128, 32], "bfloat16"),
+    "DX": ("dram", [WAVES * N, 128, 32], "bfloat16"),
+    "YS": ("dram", [WAVES * N, 128, 32], "bfloat16"),
     "YD": ("dram", [J, 128, 32], "bfloat16"),
-    "Gp": ("sbuf", [128, B], "bfloat16"),
-    "Xp": ("sbuf", [128, B], "bfloat16"),
-    "Gf": ("sbuf", [128, B], "bfloat16"),
-    "Xf": ("sbuf", [128, B], "bfloat16"),
-    "Hf": ("sbuf", [128, B], "bfloat16"),
-    "Hp": ("sbuf", [128, B], "bfloat16"),
 }
-SEMAPHORES = ["l0", "l1", "arr", "ms", "lg", "lx", "vs", "so", "snt", "ha", "hb", "st"]
+for _w in range(WAVES):
+    for _n in ("Gp", "Xp", "Gf", "Xf", "Hf", "Hp"):
+        SCRATCH["%s%d" % (_n, _w)] = ("sbuf", [128, B], "bfloat16")
+SEMAPHORES = (["ms", "vs", "snt", "st"] + ["c%d" % i for i in range(2 * J // GRP)]
+              + ["%s%d" % (n, w) for w in range(WAVES) for n in ("ag", "ax", "lg", "lx", "so", "h")])
 
 
 def owner_cores(T, topo):
@@ -29,12 +31,12 @@ def owner_cores(T, topo):
     chips = sorted({topo.chip(c) for c in cores})
     dies = sorted({topo.die(c) for c in cores})
     out = []
-    for d in dies:
-        for ch in chips:
-            ok = [c for c in cores if topo.chip(c) == ch and topo.die(c) == d and c not in T.cores
-                  and all(topo.may_write(c, t) for t in T.cores)]
-            out.append(ok[0])
-    assert len(out) == J
+    for i, ch in enumerate(chips):
+        d = dies[i % len(dies)]
+        ok = [c for c in cores if topo.chip(c) == ch and topo.die(c) == d and c not in T.cores
+              and all(topo.may_write(c, t) for t in T.cores)]
+        out.append(ok[0])
+    assert len(out) == OWN
     return out
 
 
@@ -49,45 +51,41 @@ def rank_program(g, core, T, topo):
     r = T.rank_of(core)
     sent = [0]
 
-    def fused(items, sem_of):
+    def fused(items, sem):
         m = -1
         for c, _, _, _ in items:
             assert topo.may_write(core, c)
             m &= topo.mask(core, c)
         e = [1 << i for i in range(m.bit_length()) if (m >> i) & 1]
         tr, at = [], 0
-        for i, (c, src, dst, n) in enumerate(items):
+        for c, src, dst, n in items:
             rid, pid, _ = topo.addr(c)
             tr.append(RemoteDMATransfer(dst_ids=[DstId(rid=rid, pnc=pid)], dma_engine_mask=sum(e[at:at + n]),
-                                        remote_sem=sem_of(i), src=src, dst=dst))
+                                        remote_sem=sem, src=src, dst=dst))
             at += n
             sent[0] += n
         assert at <= len(e)
         g.remote_dma_fused(tr, local_sem=S.snt)
 
     if r is not None:
-        turn = r % (J // GRP)
-        half_k, half_p = J // 2, 64
-        for j in range(2):
-            h = ((2 * j) ^ turn) // 2
-            ks, ps = slice(half_k * h, half_k * (h + 1)), slice(half_p * h, half_p * (h + 1))
-            g.sync.dma_start(out=T.XG[ks, 0:64, :], in_=T.gate[ps, :]).then_inc(S["l%d" % j], 16)
-            g.scalar.dma_start(out=T.XG[ks, 64:128, :], in_=T.x[ps, :]).then_inc(S["l%d" % j], 16)
-        for j in range(J // GRP):
-            if j % 2 == 0:
-                g.wait_ge(S["l%d" % (j // 2)], 32)
-            q = j ^ turn
-            fused([(owners[k], T.XG[k], T.D[r], 1) for k in range(GRP * q, GRP * (q + 1))], lambda i: S.arr)
-
-        def due(ks):
-            return sum(n for k in ks for call in round2_plan(k) for d, n in call if d == r)
-
-        g.sync.wait_ge(S.ha, due(range(0, half_k)))
-        g.sync.dma_start(out=T.y[0:half_p, :], in_=T.YD[0:half_k, :, :]).then_inc(S.st, 16)
-        g.scalar.wait_ge(S.hb, due(range(half_k, J)))
-        g.scalar.dma_start(out=T.y[half_p:128, :], in_=T.YD[half_k:J, :, :]).then_inc(S.st, 16)
+        rows = 128 // WAVES
+        calls = OWN // GRP
+        plan = [(w, t, (j + r) % calls) for w in range(WAVES) for t in range(2) for j in range(calls)]
+        bufs = ((T.SG, T.gate, T.DG, "ag"), (T.SX, T.x, T.DX, "ax"))
+        for i, (w, t, q) in enumerate(plan):
+            k0 = OWN * w + GRP * q
+            (g.sync, g.scalar)[i % 2].dma_start(out=bufs[t][0][k0:k0 + GRP, :, :],
+                                                in_=bufs[t][1][R * k0:R * (k0 + GRP), :]).then_inc(S["c%d" % i], 16)
+        for i, (w, t, q) in enumerate(plan):
+            g.wait_ge(S["c%d" % i], 16)
+            fused([(owners[k], bufs[t][0][OWN * w + k], bufs[t][2][N * w + r], 1)
+                   for k in range(GRP * q, GRP * (q + 1))], S["%s%d" % (bufs[t][3], w)])
+        due = sum(n for k in range(OWN) for call in round2_plan(k) for d, n in call if d == r)
+        for w, q in zip(range(WAVES), (g.sync, g.scalar)):
+            q.wait_ge(S["h%d" % w], due)
+            q.dma_start(out=T.y[rows * w:rows * (w + 1), :], in_=T.YD[OWN * w:OWN * (w + 1), :, :]).then_inc(S.st, 16)
         g.wait_ge(S.snt, sent[0])
-        g.wait_ge(S.st, 32)
+        g.wait_ge(S.st, 16 * WAVES)
         return
 
     if core not in owners:
@@ -96,33 +94,39 @@ def rank_program(g, core, T, topo):
     k = owners.index(core)
     v = g.vector
     used = 2 * N
-    v.memset(T.Gp[:, :], 0.0).then_inc(S.ms, 1)
-    v.memset(T.Xp[:, :], 0.0).then_inc(S.ms, 1)
+    for w in range(WAVES):
+        v.memset(T["Gp%d" % w][:, :], 0.0).then_inc(S.ms, 1)
+        v.memset(T["Xp%d" % w][:, :], 0.0).then_inc(S.ms, 1)
     queues = (g.sync, g.scalar)
     for q in queues:
-        q.wait_ge(S.ms, 2)
-        q.wait_ge(S.arr, N)
-    for t, (buf, sem) in enumerate(((T.Gp, S.lg), (T.Xp, S.lx))):
+        q.wait_ge(S.ms, 2 * WAVES)
+    v.wait_ge(S.ms, 2 * WAVES)
+    for w in range(WAVES):
+        for name, land, a, l in (("Gp", T.DG, "ag", "lg"), ("Xp", T.DX, "ax", "lx")):
+            for q in queues:
+                q.wait_ge(S["%s%d" % (a, w)], N)
+            for p in range(R):
+                queues[p % 2].dma_start(out=T["%s%d" % (name, w)][SLOT * p:SLOT * p + used, :],
+                                        in_=land[N * w:N * (w + 1), 32 * p:32 * (p + 1), :]
+                                        ).then_inc(S["%s%d" % (l, w)], 16)
+    for w in range(WAVES):
+        Gp, Xp, Gf, Xf, Hf, Hp = [T["%s%d" % (n, w)][:, :] for n in ("Gp", "Xp", "Gf", "Xf", "Hf", "Hp")]
+        v.wait_ge(S["lg%d" % w], 16 * R)
+        v.transpose(out=Gf, in_=Gp).then_inc(S.vs, 1)
+        v.wait_ge(S["lx%d" % w], 16 * R)
+        v.transpose(out=Xf, in_=Xp).then_inc(S.vs, 1)
+        v.wait_ge(S.vs, 4 * w + 2)
+        v.tensor_tensor_scan(out=Hf, data0=Gf, data1=Xf, initial=0.0,
+                             op0=AluOpType.mult, op1=AluOpType.add).then_inc(S.vs, 1)
+        v.wait_ge(S.vs, 4 * w + 3)
+        v.transpose(out=Hp, in_=Hf).then_inc(S.vs, 1)
+    for w in range(WAVES):
+        for q in queues:
+            q.wait_ge(S.vs, 4 * w + 4)
         for p in range(R):
-            queues[p % 2].dma_start(out=buf[SLOT * p:SLOT * p + used, :],
-                                    in_=T.D[:, 64 * t + 16 * p:64 * t + 16 * (p + 1), :]).then_inc(sem, 16)
-    v.wait_ge(S.ms, 2)
-    v.wait_ge(S.lg, 16 * R)
-    v.transpose(out=T.Gf[:, :], in_=T.Gp[:, :]).then_inc(S.vs, 1)
-    v.wait_ge(S.lx, 16 * R)
-    v.transpose(out=T.Xf[:, :], in_=T.Xp[:, :]).then_inc(S.vs, 1)
-    v.wait_ge(S.vs, 2)
-    v.tensor_tensor_scan(out=T.Hf[:, :], data0=T.Gf[:, :], data1=T.Xf[:, :], initial=0.0,
-                         op0=AluOpType.mult, op1=AluOpType.add).then_inc(S.vs, 1)
-    v.wait_ge(S.vs, 3)
-    v.transpose(out=T.Hp[:, :], in_=T.Hf[:, :]).then_inc(S.vs, 1)
-    for q in queues:
-        q.wait_ge(S.vs, 4)
-    for p in range(R):
-        queues[p % 2].dma_start(out=T.YS[:, 32 * p:32 * (p + 1), :],
-                                in_=T.Hp[SLOT * p:SLOT * p + used, :]).then_inc(S.so, 16)
-    g.wait_ge(S.so, 16 * R)
-    land = S.ha if k < J // 2 else S.hb
-    for call in round2_plan(k):
-        fused([(T.cores[d], T.YS[d], T.YD[k], n) for d, n in call], lambda i: land)
+            queues[p % 2].dma_start(out=T.YS[N * w:N * (w + 1), 32 * p:32 * (p + 1), :],
+                                    in_=T["Hp%d" % w][SLOT * p:SLOT * p + used, :]).then_inc(S["so%d" % w], 16)
+        g.wait_ge(S["so%d" % w], 16 * R)
+        for call in round2_plan(k):
+            fused([(T.cores[d], T.YS[N * w + d], T.YD[OWN * w + k], n) for d, n in call], S["h%d" % w])
     g.wait_ge(S.snt, sent[0])

@@ -4,26 +4,25 @@ from concourse.mybir import AluOpType
 N = 12
 B = 512
 CORES_ALL = 128
-J = 32
+J = 64
 WAVES = 2
 OWN = J // WAVES
 R = 128 // J
 SLOT = 32
 GRP = 8
+HALF = SLOT * R
 
 SCRATCH = {
-    "SG": ("dram", [J, 128, 32], "bfloat16"),
-    "SX": ("dram", [J, 128, 32], "bfloat16"),
-    "DG": ("dram", [WAVES * N, 128, 32], "bfloat16"),
-    "DX": ("dram", [WAVES * N, 128, 32], "bfloat16"),
-    "YS": ("dram", [WAVES * N, 128, 32], "bfloat16"),
-    "YD": ("dram", [J, 128, 32], "bfloat16"),
+    "SP": ("dram", [J, 128, 32], "bfloat16"),
+    "DP": ("dram", [WAVES * N, 128, 32], "bfloat16"),
+    "YS": ("dram", [WAVES * N, 128, 16], "bfloat16"),
+    "YD": ("dram", [J, 128, 16], "bfloat16"),
 }
 for _w in range(WAVES):
-    for _n in ("Gp", "Xp", "Gf", "Xf", "Hf", "Hp"):
+    for _n in ("Fp", "Ff", "Hf", "Hp"):
         SCRATCH["%s%d" % (_n, _w)] = ("sbuf", [128, B], "bfloat16")
-SEMAPHORES = (["ms", "vs", "snt", "st"] + ["c%d" % i for i in range(2 * J // GRP)]
-              + ["%s%d" % (n, w) for w in range(WAVES) for n in ("ag", "ax", "lg", "lx", "so", "h")])
+SEMAPHORES = (["ms", "vs", "snt", "st"] + ["c%d" % i for i in range(J // GRP)]
+              + ["%s%d" % (n, w) for w in range(WAVES) for n in ("a", "l", "so", "h")])
 
 
 def owner_cores(T, topo):
@@ -31,11 +30,11 @@ def owner_cores(T, topo):
     chips = sorted({topo.chip(c) for c in cores})
     dies = sorted({topo.die(c) for c in cores})
     out = []
-    for i, ch in enumerate(chips):
-        d = dies[i % len(dies)]
-        ok = [c for c in cores if topo.chip(c) == ch and topo.die(c) == d and c not in T.cores
-              and all(topo.may_write(c, t) for t in T.cores)]
-        out.append(ok[0])
+    for d in dies:
+        for ch in chips:
+            ok = [c for c in cores if topo.chip(c) == ch and topo.die(c) == d and c not in T.cores
+                  and all(topo.may_write(c, t) for t in T.cores)]
+            out.append(ok[0])
     assert len(out) == OWN
     return out
 
@@ -70,16 +69,17 @@ def rank_program(g, core, T, topo):
     if r is not None:
         rows = 128 // WAVES
         calls = OWN // GRP
-        plan = [(w, t, (j + r) % calls) for w in range(WAVES) for t in range(2) for j in range(calls)]
-        bufs = ((T.SG, T.gate, T.DG, "ag"), (T.SX, T.x, T.DX, "ax"))
-        for i, (w, t, q) in enumerate(plan):
+        plan = [(w, (j + r) % calls) for w in range(WAVES) for j in range(calls)]
+        for i, (w, q) in enumerate(plan):
             k0 = OWN * w + GRP * q
-            (g.sync, g.scalar)[i % 2].dma_start(out=bufs[t][0][k0:k0 + GRP, :, :],
-                                                in_=bufs[t][1][R * k0:R * (k0 + GRP), :]).then_inc(S["c%d" % i], 16)
-        for i, (w, t, q) in enumerate(plan):
-            g.wait_ge(S["c%d" % i], 16)
-            fused([(owners[k], bufs[t][0][OWN * w + k], bufs[t][2][N * w + r], 1)
-                   for k in range(GRP * q, GRP * (q + 1))], S["%s%d" % (bufs[t][3], w)])
+            g.sync.dma_start(out=T.SP[k0:k0 + GRP, 0:64, :],
+                             in_=T.gate[R * k0:R * (k0 + GRP), :]).then_inc(S["c%d" % i], 16)
+            g.scalar.dma_start(out=T.SP[k0:k0 + GRP, 64:128, :],
+                               in_=T.x[R * k0:R * (k0 + GRP), :]).then_inc(S["c%d" % i], 16)
+        for i, (w, q) in enumerate(plan):
+            g.wait_ge(S["c%d" % i], 32)
+            fused([(owners[k], T.SP[OWN * w + k], T.DP[N * w + r], 1)
+                   for k in range(GRP * q, GRP * (q + 1))], S["a%d" % w])
         due = sum(n for k in range(OWN) for call in round2_plan(k) for d, n in call if d == r)
         for w, q in zip(range(WAVES), (g.sync, g.scalar)):
             q.wait_ge(S["h%d" % w], due)
@@ -95,36 +95,31 @@ def rank_program(g, core, T, topo):
     v = g.vector
     used = 2 * N
     for w in range(WAVES):
-        v.memset(T["Gp%d" % w][:, :], 0.0).then_inc(S.ms, 1)
-        v.memset(T["Xp%d" % w][:, :], 0.0).then_inc(S.ms, 1)
+        v.memset(T["Fp%d" % w][:, :], 0.0).then_inc(S.ms, 1)
     queues = (g.sync, g.scalar)
     for q in queues:
-        q.wait_ge(S.ms, 2 * WAVES)
-    v.wait_ge(S.ms, 2 * WAVES)
-    for w in range(WAVES):
-        for name, land, a, l in (("Gp", T.DG, "ag", "lg"), ("Xp", T.DX, "ax", "lx")):
-            for q in queues:
-                q.wait_ge(S["%s%d" % (a, w)], N)
-            for p in range(R):
-                queues[p % 2].dma_start(out=T["%s%d" % (name, w)][SLOT * p:SLOT * p + used, :],
-                                        in_=land[N * w:N * (w + 1), 32 * p:32 * (p + 1), :]
-                                        ).then_inc(S["%s%d" % (l, w)], 16)
-    for w in range(WAVES):
-        Gp, Xp, Gf, Xf, Hf, Hp = [T["%s%d" % (n, w)][:, :] for n in ("Gp", "Xp", "Gf", "Xf", "Hf", "Hp")]
-        v.wait_ge(S["lg%d" % w], 16 * R)
-        v.transpose(out=Gf, in_=Gp).then_inc(S.vs, 1)
-        v.wait_ge(S["lx%d" % w], 16 * R)
-        v.transpose(out=Xf, in_=Xp).then_inc(S.vs, 1)
-        v.wait_ge(S.vs, 4 * w + 2)
-        v.tensor_tensor_scan(out=Hf, data0=Gf, data1=Xf, initial=0.0,
-                             op0=AluOpType.mult, op1=AluOpType.add).then_inc(S.vs, 1)
-        v.wait_ge(S.vs, 4 * w + 3)
-        v.transpose(out=Hp, in_=Hf).then_inc(S.vs, 1)
+        q.wait_ge(S.ms, WAVES)
+    v.wait_ge(S.ms, WAVES)
     for w in range(WAVES):
         for q in queues:
-            q.wait_ge(S.vs, 4 * w + 4)
+            q.wait_ge(S["a%d" % w], N)
+        for j in range(2 * R):
+            queues[j % 2].dma_start(out=T["Fp%d" % w][SLOT * j:SLOT * j + used, :],
+                                    in_=T.DP[N * w:N * (w + 1), 32 * j:32 * (j + 1), :]).then_inc(S["l%d" % w], 16)
+    for w in range(WAVES):
+        Fp, Ff, Hf, Hp = [T["%s%d" % (n, w)] for n in ("Fp", "Ff", "Hf", "Hp")]
+        v.wait_ge(S["l%d" % w], 16 * 2 * R)
+        v.transpose(out=Ff[:, :], in_=Fp[:, :]).then_inc(S.vs, 1)
+        v.wait_ge(S.vs, 3 * w + 1)
+        v.tensor_tensor_scan(out=Hf[0:HALF, :], data0=Ff[0:HALF, :], data1=Ff[HALF:2 * HALF, :], initial=0.0,
+                             op0=AluOpType.mult, op1=AluOpType.add).then_inc(S.vs, 1)
+        v.wait_ge(S.vs, 3 * w + 2)
+        v.transpose(out=Hp[0:HALF, :], in_=Hf[0:HALF, :]).then_inc(S.vs, 1)
+    for w in range(WAVES):
+        for q in queues:
+            q.wait_ge(S.vs, 3 * w + 3)
         for p in range(R):
-            queues[p % 2].dma_start(out=T.YS[N * w:N * (w + 1), 32 * p:32 * (p + 1), :],
+            queues[p % 2].dma_start(out=T.YS[N * w:N * (w + 1), 64 * p:64 * (p + 1), :],
                                     in_=T["Hp%d" % w][SLOT * p:SLOT * p + used, :]).then_inc(S["so%d" % w], 16)
         g.wait_ge(S["so%d" % w], 16 * R)
         for call in round2_plan(k):

from concourse.bass import DstId, RemoteDMATransfer
from concourse.mybir import AluOpType

N = 12
B = 512
CORES_ALL = 128
J = 64
WAVES = 2
OWN = J // WAVES
R = 128 // J
SLOT = 32
GRP = 8
HALF = SLOT * R

SCRATCH = {
    "SP": ("dram", [J, 128, 32], "bfloat16"),
    "DP": ("dram", [WAVES * N, 128, 32], "bfloat16"),
    "YS": ("dram", [WAVES * N, 128, 16], "bfloat16"),
    "YD": ("dram", [J, 128, 16], "bfloat16"),
}
for _w in range(WAVES):
    for _n in ("Fp", "Ff", "Hf", "Hp"):
        SCRATCH["%s%d" % (_n, _w)] = ("sbuf", [128, B], "bfloat16")
SEMAPHORES = (["ms", "vs", "snt", "st"] + ["c%d" % i for i in range(J // GRP)]
              + ["%s%d" % (n, w) for w in range(WAVES) for n in ("a", "l", "so", "h")])


def owner_cores(T, topo):
    cores = list(range(CORES_ALL))
    chips = sorted({topo.chip(c) for c in cores})
    dies = sorted({topo.die(c) for c in cores})
    out = []
    for d in dies:
        for ch in chips:
            ok = [c for c in cores if topo.chip(c) == ch and topo.die(c) == d and c not in T.cores
                  and all(topo.may_write(c, t) for t in T.cores)]
            out.append(ok[0])
    assert len(out) == OWN
    return out


def round2_plan(k):
    order = [(k + j) % N for j in range(N)]
    return [[(d, 1) for d in order[:8]], [(d, 2) for d in order[8:]]]


def rank_program(g, core, T, topo):
    S = T.sem
    owners = owner_cores(T, topo)
    r = T.rank_of(core)
    sent = [0]

    def fused(items, sem):
        m = -1
        for c, _, _, _ in items:
            assert topo.may_write(core, c)
            m &= topo.mask(core, c)
        e = [1 << i for i in range(m.bit_length()) if (m >> i) & 1]
        tr, at = [], 0
        for c, src, dst, n in items:
            rid, pid, _ = topo.addr(c)
            tr.append(RemoteDMATransfer(dst_ids=[DstId(rid=rid, pnc=pid)], dma_engine_mask=sum(e[at:at + n]),
                                        remote_sem=sem, src=src, dst=dst))
            at += n
            sent[0] += n
        assert at <= len(e)
        g.remote_dma_fused(tr, local_sem=S.snt)

    if r is not None:
        rows = 128 // WAVES
        calls = OWN // GRP
        plan = [(w, (j + r) % calls) for w in range(WAVES) for j in range(calls)]
        for i, (w, q) in enumerate(plan):
            k0 = OWN * w + GRP * q
            g.sync.dma_start(out=T.SP[k0:k0 + GRP, 0:64, :],
                             in_=T.gate[R * k0:R * (k0 + GRP), :]).then_inc(S["c%d" % i], 16)
            g.scalar.dma_start(out=T.SP[k0:k0 + GRP, 64:128, :],
                               in_=T.x[R * k0:R * (k0 + GRP), :]).then_inc(S["c%d" % i], 16)
        for i, (w, q) in enumerate(plan):
            g.wait_ge(S["c%d" % i], 32)
            fused([(owners[k], T.SP[OWN * w + k], T.DP[N * w + r], 1)
                   for k in range(GRP * q, GRP * (q + 1))], S["a%d" % w])
        due = sum(n for k in range(OWN) for call in round2_plan(k) for d, n in call if d == r)
        for w, q in zip(range(WAVES), (g.sync, g.scalar)):
            q.wait_ge(S["h%d" % w], due)
            q.dma_start(out=T.y[rows * w:rows * (w + 1), :], in_=T.YD[OWN * w:OWN * (w + 1), :, :]).then_inc(S.st, 16)
        g.wait_ge(S.snt, sent[0])
        g.wait_ge(S.st, 16 * WAVES)
        return

    if core not in owners:
        return

    k = owners.index(core)
    v = g.vector
    used = 2 * N
    for w in range(WAVES):
        v.memset(T["Fp%d" % w][:, :], 0.0).then_inc(S.ms, 1)
    queues = (g.sync, g.scalar)
    for q in queues:
        q.wait_ge(S.ms, WAVES)
    v.wait_ge(S.ms, WAVES)
    for w in range(WAVES):
        for q in queues:
            q.wait_ge(S["a%d" % w], N)
        for j in range(2 * R):
            queues[j % 2].dma_start(out=T["Fp%d" % w][SLOT * j:SLOT * j + used, :],
                                    in_=T.DP[N * w:N * (w + 1), 32 * j:32 * (j + 1), :]).then_inc(S["l%d" % w], 16)
    for w in range(WAVES):
        Fp, Ff, Hf, Hp = [T["%s%d" % (n, w)] for n in ("Fp", "Ff", "Hf", "Hp")]
        v.wait_ge(S["l%d" % w], 16 * 2 * R)
        v.transpose(out=Ff[:, :], in_=Fp[:, :]).then_inc(S.vs, 1)
        v.wait_ge(S.vs, 3 * w + 1)
        v.tensor_tensor_scan(out=Hf[0:HALF, :], data0=Ff[0:HALF, :], data1=Ff[HALF:2 * HALF, :], initial=0.0,
                             op0=AluOpType.mult, op1=AluOpType.add).then_inc(S.vs, 1)
        v.wait_ge(S.vs, 3 * w + 2)
        v.transpose(out=Hp[0:HALF, :], in_=Hf[0:HALF, :]).then_inc(S.vs, 1)
    for w in range(WAVES):
        for q in queues:
            q.wait_ge(S.vs, 3 * w + 3)
        for p in range(R):
            queues[p % 2].dma_start(out=T.YS[N * w:N * (w + 1), 64 * p:64 * (p + 1), :],
                                    in_=T["Hp%d" % w][SLOT * p:SLOT * p + used, :]).then_inc(S["so%d" % w], 16)
        g.wait_ge(S["so%d" % w], 16 * R)
        for call in round2_plan(k):
            fused([(T.cores[d], T.YS[N * w + d], T.YD[OWN * w + k], n) for d, n in call], S["h%d" % w])
    g.wait_ge(S.snt, sent[0])
